import numpy as np
import ml_dtypes


def mxq(x, axis, fmt="e4m3"):
    dtype, down = {"e4m3": (ml_dtypes.float8_e4m3fn, 7), "e5m2": (ml_dtypes.float8_e5m2, 14)}[fmt]
    v = np.moveaxis(np.asarray(x, np.float32).astype(ml_dtypes.bfloat16).astype(np.float64), axis, -1)
    blocks = v.reshape(v.shape[:-1] + (-1, 32))
    amax = np.abs(blocks).max(-1, keepdims=True)
    byte = np.maximum(np.where(amax > 0, np.frexp(amax)[1] - 1 + 127, 0) - down, 1)
    scale = np.exp2(byte - 127.0)
    codes = (blocks / scale).astype(np.float32).astype(dtype).astype(np.float64)
    return np.moveaxis((codes * scale).reshape(v.shape), -1, axis)


WIDE = False


def mx_kscale(k):
    if not WIDE:
        return np.ones(k)
    levels = np.array([10, -10, 5, -5, 0])
    if k % 512:
        return np.exp2(np.random.permutation(np.resize(levels, k // 32))).repeat(32)
    a = np.empty((k // 512, 16))
    for p in range(k // 512):
        a[p, :8] = np.random.permutation(np.resize(levels, 8))
        for g in range(8):
            far = levels[np.abs(levels - a[p, g]) >= 10]
            a[p, g + 8] = far[np.random.randint(len(far))]
    return np.exp2(a.ravel()).repeat(32)


def f64(x):
    return np.asarray(x).astype(np.float64)


def striped(idx):
    return np.tile(np.asarray(idx).reshape(-1, 16).T, (8, 1)).astype(np.uint16)


def unstriped(offs):
    return offs[:16].T.reshape(-1).astype(np.int64)


E2M1 = np.array([0.0, 0.5, 1.0, 1.5, 2.0, 3.0, 4.0, 6.0, -0.0, -0.5, -1.0, -1.5, -2.0, -3.0, -4.0, -6.0])


def pack_weight(w, fmt):
    k, n = w.shape
    w = f64(np.asarray(w, np.float32).astype(ml_dtypes.bfloat16)).reshape(k // 32, 32, n)
    amax = np.abs(w).max(1)
    if fmt == "e4m3":
        byte = np.frexp(amax)[1] - 1 + 127 - 7
    else:
        mant, ex = np.frexp(amax / 6.0)
        byte = np.where(mant > 0.5, ex, ex - 1) + 127
    byte = np.clip(np.where(amax > 0, byte, 1), 1, 254)
    scaled = (w * np.exp2(127.0 - byte)[:, None, :]).reshape(k, n).astype(np.float32)
    by_word = np.ascontiguousarray(scaled.reshape(k // 512, 128, 4, n).transpose(0, 1, 3, 2))
    if fmt == "e4m3":
        words = by_word.astype(ml_dtypes.float8_e4m3fn).view(np.uint8)
    else:
        c = by_word.astype(ml_dtypes.float4_e2m1fn).view(np.uint8) & 0xF
        words = (c[..., 0::2] | (c[..., 1::2] << 4)).reshape(k // 512, 128, 2 * n)
    return np.ascontiguousarray(words), np.ascontiguousarray(byte.astype(np.uint8).reshape(k // 512, 16, n))


def unpack_weight(words, scales, fmt):
    g, _, n = scales.shape
    words = np.ascontiguousarray(words).reshape(g, 128, n, -1)
    if fmt == "e4m3":
        vals = words.view(ml_dtypes.float8_e4m3fn).astype(np.float64)
    else:
        nib = np.empty((g, 128, n, 4), np.uint8)
        nib[..., 0::2] = words & 0xF
        nib[..., 1::2] = words >> 4
        vals = E2M1[nib]
    vals = vals * np.repeat(np.exp2(scales.astype(np.float64) - 127.0), 8, axis=1)[..., None]
    return vals.transpose(0, 1, 3, 2).reshape(g * 512, n)


def sigmoid(v):
    return 1.0 / (1.0 + np.exp(-v))


B, N, T, D, NQ = 1, 512, 2048, 512, 512
SEG = 32


def setup_inputs():
    n = np.random.standard_normal
    idx = np.random.permutation(T)[:B * N]
    s = mx_kscale(D)[:, None]
    kp = pack_weight(n((D, T)) / s, "e4m3")
    return {
        "qT": (n((B, D, NQ)) * s * (1.00 / np.sqrt(D))).astype(np.float32),
        "k_words": kp[0],
        "k_scales": kp[1],
        "th": (n((B, 1, NQ)) + 1).astype(np.float32),
        "offs": striped(idx),
    }


def reference(qT, k_words, k_scales, th, offs):
    idx = unstriped(offs)
    pick = lambda x, which: x[:, which].reshape(x.shape[0], B, -1).transpose(1, 0, 2)
    k = unpack_weight(k_words, k_scales, "e4m3")
    kg = pick(k, idx)
    qq = mxq(f64(qT), 1, "e4m3")
    a = kg.transpose(0, 2, 1) @ qq
    y = sigmoid(8.0 * (a - f64(th))).reshape(B, N, NQ // SEG, SEG).sum(-1)
    return y

@@ -1,0 +1,175 @@
+from contextlib import ExitStack
+
+import concourse.mybir as mybir
+from concourse.masks import make_identity
+
+N, T, D, NQ, SEG = 512, 2048, 512, 512, 32
+FLOPS = 2 * N * D * NQ
+
+F32 = mybir.dt.float32
+BF16 = mybir.dt.bfloat16
+I32 = mybir.dt.int32
+U32 = mybir.dt.uint32
+U16 = mybir.dt.uint16
+U8 = mybir.dt.uint8
+FP8X4 = mybir.dt.float8_e4m3fn_x4
+SIGMOID = mybir.ActivationFunctionType.Sigmoid
+ADD = mybir.AluOpType.add
+MULT = mybir.AluOpType.mult
+AXIS_X = mybir.AxisListType.X
+
+P = 128
+PACK = 4
+HALF = N // 2
+RUNS = NQ // SEG
+GAIN = 8.0
+
+
+def tile_attend_tok_vote_topk_kernel(tc, qT, k_words, k_scales, th, offs, out):
+    nc = tc.nc
+    with ExitStack() as ctx:
+        sb = ctx.enter_context(tc.tile_pool(name="sb", bufs=1))
+        ps = ctx.enter_context(tc.psum_pool(name="ps", bufs=1))
+        banks = [ps.tile([P, 512], F32, name=f"bank{b}") for b in range(7)]
+
+        offsets = sb.tile([P, N // 16], U16, name="offsets")
+        nc.sync.dma_start(offsets[:], offs)
+
+        q_rows = qT[0].rearrange("(p j) q -> p j q", j=PACK)
+        raw_pair = sb.tile([P, PACK, 2 * P], F32, name="raw_pair", tag="raw")
+        nc.sync.dma_start(raw_pair[:], q_rows[:, :, 0 : 2 * P])
+
+        th_rows = sb.tile([P, 2 * P], F32, name="th_rows")
+        nc.vector.memset(th_rows[:], 0.0)
+        nc.scalar.dma_start(th_rows[0:2, :], th[0, 0].rearrange("(c q) -> c q", c=2))
+
+        pool_scales = sb.tile([P, T // 4], I32, name="pool_scales")
+        nc.vector.memset(pool_scales[:], 0)
+        scale_rows = k_scales[0].bitcast(I32)
+        for quad in range(4):
+            nc.scalar.dma_start(pool_scales[32 * quad : 32 * quad + 4, :], scale_rows[4 * quad : 4 * quad + 4, :])
+
+        pool_words = sb.tile([P, T], I32, name="pool_words")
+        nc.sync.dma_start(pool_words[:], k_words[0].rearrange("p t r -> p (t r)").bitcast(I32))
+
+        raw_late = [sb.tile([P, PACK, P], F32, name="raw_late0")]
+        nc.sync.dma_start(raw_late[0][:], q_rows[:, :, 2 * P : 3 * P])
+
+        ident = sb.tile([P, P], F32, name="ident")
+        make_identity(nc, ident[:])
+
+        grouped_pair = sb.tile([P, 2, P, PACK], BF16, name="grouped_pair", align_bytes=64)
+        nc.vector.tensor_copy(grouped_pair[:], raw_pair[:].rearrange("p j (m e) -> p e m j", e=2))
+
+        raw_late.append(sb.tile([P, PACK, P], F32, name="raw_late1", tag="raw"))
+        nc.sync.dma_start(raw_late[1][:], q_rows[:, :, 3 * P : 4 * P])
+
+        key_scales = sb.tile([P, N], U8, name="key_scales", align_bytes=64)
+        nc.vector.tensor_copy(key_scales[:], pool_scales[:].bitcast(U8).indirect(offsets[:]))
+
+        codes_pair = sb.tile([P, 2 * P], U32, name="codes_pair", align_bytes=64)
+        scales_pair = sb.tile([P, 2 * P], U8, name="scales_pair", align_bytes=64)
+        nc.vector.quantize_mx(
+            out=codes_pair[:].bitcast(FP8X4),
+            scales=scales_pair[:],
+            in_=grouped_pair[:].rearrange("p e m j -> p (e m j)"),
+        )
+
+        th_views = [th_rows[:, 0 : 2 * P : 2], th_rows[:, 1 : 2 * P : 2], th_rows[:, 0:P], th_rows[:, P : 2 * P]]
+        for t in range(4):
+            nc.tensor.transpose(banks[0][:, t * P : (t + 1) * P], th_views[t], ident[:])
+        bias = sb.tile([P, 4], F32, name="bias")
+        th_cols = banks[0][:].rearrange("p (t c) -> p t c", t=4)
+        for c in range(2):
+            nc.vector.tensor_scalar(bias[:, 2 * c : 2 * c + 2], th_cols[:, 2 * c : 2 * c + 2, c], -GAIN, None, MULT)
+
+        key_words = [sb.tile([P, HALF], U32, name=f"key_words{h}", align_bytes=64) for h in range(2)]
+        for h in range(2):
+            nc.vector.tensor_copy(key_words[h][:], pool_words[:].bitcast(U32).indirect(offsets[:, 16 * h : 16 * h + 16]))
+
+        def scores(bank, codes, scales, h):
+            nc.tensor.matmul_mx(
+                out=bank[:, h * HALF : (h + 1) * HALF],
+                lhsT=codes.bitcast(FP8X4),
+                lhsT_scale=scales,
+                rhs=key_words[h][:].bitcast(FP8X4),
+                rhs_scale=key_scales[:, h * HALF : (h + 1) * HALF],
+                start=True,
+                stop=True,
+            )
+
+        def votes(bank, t, h):
+            vote = sb.tile([P, 2, P], F32, name=f"vote{t}_{h}")
+            nc.scalar.activation(
+                vote[:],
+                bank[:, h * HALF : (h + 1) * HALF].rearrange("p (k e) -> p e k", e=2),
+                SIGMOID,
+                bias=bias[:, t : t + 1],
+                scale=GAIN,
+            )
+            return vote
+
+        def turn(bank, col, vote, start, stop):
+            nc.tensor.matmul(bank[:, col * P : (col + 1) * P], lhsT=vote, rhs=ident[:], is_transpose=True, start=start, stop=stop)
+
+        def quantize_late(u):
+            grouped = sb.tile([P, P, PACK], BF16, name=f"grouped_late{u}", align_bytes=64)
+            nc.vector.tensor_copy(
+                grouped[:].rearrange("p (c i) j -> p c j i", i=4),
+                raw_late[u][:].rearrange("p j (c i) -> p c j i", i=4),
+            )
+            codes = sb.tile([P, P], U32, name=f"codes_late{u}", align_bytes=64)
+            scales = sb.tile([P, P], U8, name=f"scales_late{u}", align_bytes=64)
+            nc.vector.quantize_mx(out=codes[:].bitcast(FP8X4), scales=scales[:], in_=grouped[:].rearrange("p m j -> p (m j)"))
+            return codes, scales
+
+        res = sb.tile([P, 2, 2, RUNS], F32, name="res")
+        out_rows = out[0].rearrange("(h p e) j -> h p (e j)", h=2, e=2)
+
+        for h in range(2):
+            for e in range(2):
+                scores(banks[1 + 2 * h + e], codes_pair[:, e * P : (e + 1) * P], scales_pair[:, e * P : (e + 1) * P], h)
+        pair_votes = [[votes(banks[1 + 2 * h + e], e, h) for e in range(2)] for h in range(2)]
+
+        codes2, scales2 = quantize_late(0)
+        for col in range(2):
+            for e in range(2):
+                turn(banks[0], col, pair_votes[0][e][:, col, :], e == 0, e == 1)
+        for h in range(2):
+            scores(banks[1 + h], codes2[:], scales2[:], h)
+        votes2 = [votes(banks[1 + h], 2, h) for h in range(2)]
+        for col in range(2):
+            for e in range(2):
+                turn(banks[0], 2 + col, pair_votes[1][e][:, col, :], e == 0, e == 1)
+
+        codes3, scales3 = quantize_late(1)
+        for h in range(2):
+            scores(banks[3 + h], codes3[:], scales3[:], h)
+        votes3 = [votes(banks[3 + h], 3, h) for h in range(2)]
+
+        nc.vector.tensor_reduce(
+            res[:].rearrange("p h e j -> p (h e) j")[:, :, 0:8],
+            banks[0][:].rearrange("p (b r u) -> p b r u", b=4, u=16),
+            AXIS_X,
+            ADD,
+        )
+        for h in range(2):
+            for col in range(2):
+                turn(banks[5], 2 * h + col, votes2[h][:, col, :], True, True)
+        nc.vector.tensor_reduce(
+            res[:].rearrange("p h e j -> p (h e) j")[:, :, 8:12],
+            banks[5][:].rearrange("p (b r u) -> p b r u", b=4, u=SEG),
+            AXIS_X,
+            ADD,
+        )
+        for h in range(2):
+            bank = banks[6] if h == 0 else banks[1]
+            for col in range(2):
+                turn(bank, col, votes3[h][:, col, :], True, True)
+            nc.vector.tensor_reduce(
+                res[:, h, :, 12:16],
+                bank[:, 0:HALF].rearrange("p (b r u) -> p b r u", b=2, u=SEG),
+                AXIS_X,
+                ADD,
+            )
+            nc.sync.dma_start(out_rows[h], res[:, h].rearrange("p e j -> p (e j)"))

@@ -14,8 +14,8 @@ U16 = mybir.dt.uint16
 U8 = mybir.dt.uint8
 FP8X4 = mybir.dt.float8_e4m3fn_x4
 SIGMOID = mybir.ActivationFunctionType.Sigmoid
+COPY = mybir.ActivationFunctionType.Copy
 ADD = mybir.AluOpType.add
-MULT = mybir.AluOpType.mult
 AXIS_X = mybir.AxisListType.X
 
 P = 128
@@ -23,6 +23,8 @@ PACK = 4
 HALF = N // 2
 RUNS = NQ // SEG
 GAIN = 8.0
+WARM_EARLY = 20
+WARM_LATE = 6
 
 
 def tile_attend_tok_vote_topk_kernel(tc, qT, k_words, k_scales, th, offs, out):
@@ -30,81 +32,83 @@ def tile_attend_tok_vote_topk_kernel(tc, qT, k_words, k_scales, th, offs, out):
     with ExitStack() as ctx:
         sb = ctx.enter_context(tc.tile_pool(name="sb", bufs=1))
         ps = ctx.enter_context(tc.psum_pool(name="ps", bufs=1))
-        banks = [ps.tile([P, 512], F32, name=f"bank{b}") for b in range(7)]
+        banks = [ps.tile([P, 512], F32, name=f"bank{b}") for b in range(8)]
 
         offsets = sb.tile([P, N // 16], U16, name="offsets")
         nc.sync.dma_start(offsets[:], offs)
-
-        q_rows = qT[0].rearrange("(p j) q -> p j q", j=PACK)
-        raw_pair = sb.tile([P, PACK, 2 * P], F32, name="raw_pair", tag="raw")
-        nc.sync.dma_start(raw_pair[:], q_rows[:, :, 0 : 2 * P])
-
-        th_rows = sb.tile([P, 2 * P], F32, name="th_rows")
-        nc.vector.memset(th_rows[:], 0.0)
-        nc.scalar.dma_start(th_rows[0:2, :], th[0, 0].rearrange("(c q) -> c q", c=2))
+        pool_words = sb.tile([P, T], I32, name="pool_words")
+        nc.sync.dma_start(pool_words[:], k_words[0].rearrange("p t r -> p (t r)").bitcast(I32))
 
         pool_scales = sb.tile([P, T // 4], I32, name="pool_scales")
         nc.vector.memset(pool_scales[:], 0)
         scale_rows = k_scales[0].bitcast(I32)
-        for quad in range(4):
-            nc.scalar.dma_start(pool_scales[32 * quad : 32 * quad + 4, :], scale_rows[4 * quad : 4 * quad + 4, :])
+        for r in range(4):
+            nc.sync.dma_start(pool_scales[r:P:32, :], scale_rows[r:16:4, :])
 
-        pool_words = sb.tile([P, T], I32, name="pool_words")
-        nc.sync.dma_start(pool_words[:], k_words[0].rearrange("p t r -> p (t r)").bitcast(I32))
+        q_rows = qT[0].rearrange("(p j) q -> p j q", j=PACK)
+        raw = [sb.tile([P, PACK, 2 * P], F32, name=f"raw{c}") for c in range(2)]
+        for c in range(2):
+            nc.sync.dma_start(raw[c][:], q_rows[:, :, 2 * P * c : 2 * P * (c + 1)])
 
-        raw_late = [sb.tile([P, PACK, P], F32, name="raw_late0")]
-        nc.sync.dma_start(raw_late[0][:], q_rows[:, :, 2 * P : 3 * P])
-
+        th_raw = sb.tile([2, 2 * P], F32, name="th_raw")
+        nc.scalar.dma_start(th_raw[:], th[0, 0].rearrange("(c q) -> c q", c=2))
+        th_rows = sb.tile([P, 2 * P], F32, name="th_rows")
+        nc.gpsimd.memset(th_rows[:], 0.0)
         ident = sb.tile([P, P], F32, name="ident")
         make_identity(nc, ident[:])
+        warm = sb.tile([P, 1], F32, name="warm")
+        nc.scalar.activation(warm[:], th_rows[:, 0:1], SIGMOID)
+        nc.scalar.activation(
+            th_rows[0:2, :].rearrange("c (e g i) -> c e g i", e=2, i=4),
+            th_raw[:].rearrange("c (g e i) -> c e g i", e=2, i=4),
+            COPY,
+            scale=-GAIN,
+        )
+        for e in range(2):
+            nc.tensor.transpose(banks[7][:, e * P : (e + 1) * P], th_rows[:, e * P : (e + 1) * P], ident[:])
+        bias = sb.tile([P, 2, 2], F32, name="bias")
+        nc.scalar.copy(bias[:], banks[7][:, 0 : 2 * P].rearrange("p (e c) -> p e c", e=2)[:, :, 0:2])
+        for w in range(WARM_EARLY):
+            nc.tensor.transpose(banks[6][:, (w % 4) * P : (w % 4 + 1) * P], th_rows[:, 0:P], ident[:])
+        for w in range(WARM_LATE):
+            nc.tensor.transpose(banks[6][:, (w % 4) * P : (w % 4 + 1) * P], raw[0][:, 0, 0:P], ident[:])
 
-        grouped_pair = sb.tile([P, 2, P, PACK], BF16, name="grouped_pair", align_bytes=64)
-        nc.vector.tensor_copy(grouped_pair[:], raw_pair[:].rearrange("p j (m e) -> p e m j", e=2))
-
-        raw_late.append(sb.tile([P, PACK, P], F32, name="raw_late1", tag="raw"))
-        nc.sync.dma_start(raw_late[1][:], q_rows[:, :, 3 * P : 4 * P])
-
+        key_words = sb.tile([P, N], U32, name="key_words", align_bytes=64)
+        nc.vector.tensor_copy(key_words[:], pool_words[:].bitcast(U32).indirect(offsets[:]))
         key_scales = sb.tile([P, N], U8, name="key_scales", align_bytes=64)
         nc.vector.tensor_copy(key_scales[:], pool_scales[:].bitcast(U8).indirect(offsets[:]))
 
-        codes_pair = sb.tile([P, 2 * P], U32, name="codes_pair", align_bytes=64)
-        scales_pair = sb.tile([P, 2 * P], U8, name="scales_pair", align_bytes=64)
-        nc.vector.quantize_mx(
-            out=codes_pair[:].bitcast(FP8X4),
-            scales=scales_pair[:],
-            in_=grouped_pair[:].rearrange("p e m j -> p (e m j)"),
-        )
+        def interleave(t, copy):
+            grouped = sb.tile([P, P, PACK], BF16, name=f"grouped{t}", align_bytes=64)
+            copy(
+                grouped[:].rearrange("p (g i) j -> p g j i", i=4),
+                raw[t // 2][:].rearrange("p j (g e i) -> p e g j i", e=2, i=4)[:, t % 2],
+            )
+            return grouped
 
-        th_views = [th_rows[:, 0 : 2 * P : 2], th_rows[:, 1 : 2 * P : 2], th_rows[:, 0:P], th_rows[:, P : 2 * P]]
-        for t in range(4):
-            nc.tensor.transpose(banks[0][:, t * P : (t + 1) * P], th_views[t], ident[:])
-        bias = sb.tile([P, 4], F32, name="bias")
-        th_cols = banks[0][:].rearrange("p (t c) -> p t c", t=4)
-        for c in range(2):
-            nc.vector.tensor_scalar(bias[:, 2 * c : 2 * c + 2], th_cols[:, 2 * c : 2 * c + 2, c], -GAIN, None, MULT)
+        def quantize(t, grouped):
+            codes = sb.tile([P, P], U32, name=f"codes{t}", align_bytes=64)
+            scales = sb.tile([P, P], U8, name=f"scales{t}", align_bytes=64)
+            nc.vector.quantize_mx(out=codes[:].bitcast(FP8X4), scales=scales[:], in_=grouped[:].rearrange("p m j -> p (m j)"))
+            return codes, scales
 
-        key_words = [sb.tile([P, HALF], U32, name=f"key_words{h}", align_bytes=64) for h in range(2)]
-        for h in range(2):
-            nc.vector.tensor_copy(key_words[h][:], pool_words[:].bitcast(U32).indirect(offsets[:, 16 * h : 16 * h + 16]))
-
-        def scores(bank, codes, scales, h):
+        def votes(t, bank, quantized, halves):
+            cols = slice(halves[0] * HALF, (halves[-1] + 1) * HALF)
             nc.tensor.matmul_mx(
-                out=bank[:, h * HALF : (h + 1) * HALF],
-                lhsT=codes.bitcast(FP8X4),
-                lhsT_scale=scales,
-                rhs=key_words[h][:].bitcast(FP8X4),
-                rhs_scale=key_scales[:, h * HALF : (h + 1) * HALF],
+                out=bank[:, cols],
+                lhsT=quantized[0][:].bitcast(FP8X4),
+                lhsT_scale=quantized[1][:],
+                rhs=key_words[:, cols].bitcast(FP8X4),
+                rhs_scale=key_scales[:, cols],
                 start=True,
                 stop=True,
             )
-
-        def votes(bank, t, h):
-            vote = sb.tile([P, 2, P], F32, name=f"vote{t}_{h}")
+            vote = sb.tile([P, len(halves), 2, P], F32, name=f"vote{t}_{halves[0]}")
             nc.scalar.activation(
                 vote[:],
-                bank[:, h * HALF : (h + 1) * HALF].rearrange("p (k e) -> p e k", e=2),
+                bank[:, cols].rearrange("p (h k s) -> p h s k", h=len(halves), s=2),
                 SIGMOID,
-                bias=bias[:, t : t + 1],
+                bias=bias[:, t % 2, t // 2 : t // 2 + 1],
                 scale=GAIN,
             )
             return vote
@@ -112,64 +116,41 @@ def tile_attend_tok_vote_topk_kernel(tc, qT, k_words, k_scales, th, offs, out):
         def turn(bank, col, vote, start, stop):
             nc.tensor.matmul(bank[:, col * P : (col + 1) * P], lhsT=vote, rhs=ident[:], is_transpose=True, start=start, stop=stop)
 
-        def quantize_late(u):
-            grouped = sb.tile([P, P, PACK], BF16, name=f"grouped_late{u}", align_bytes=64)
-            nc.vector.tensor_copy(
-                grouped[:].rearrange("p (c i) j -> p c j i", i=4),
-                raw_late[u][:].rearrange("p j (c i) -> p c j i", i=4),
-            )
-            codes = sb.tile([P, P], U32, name=f"codes_late{u}", align_bytes=64)
-            scales = sb.tile([P, P], U8, name=f"scales_late{u}", align_bytes=64)
-            nc.vector.quantize_mx(out=codes[:].bitcast(FP8X4), scales=scales[:], in_=grouped[:].rearrange("p m j -> p (m j)"))
-            return codes, scales
-
         res = sb.tile([P, 2, 2, RUNS], F32, name="res")
-        out_rows = out[0].rearrange("(h p e) j -> h p (e j)", h=2, e=2)
+        out_rows = out[0].rearrange("(h p s) j -> h p (s j)", h=2, s=2)
 
-        for h in range(2):
-            for e in range(2):
-                scores(banks[1 + 2 * h + e], codes_pair[:, e * P : (e + 1) * P], scales_pair[:, e * P : (e + 1) * P], h)
-        pair_votes = [[votes(banks[1 + 2 * h + e], e, h) for e in range(2)] for h in range(2)]
+        grouped0 = interleave(0, nc.scalar.copy)
+        grouped1 = interleave(1, nc.scalar.copy)
+        q0 = quantize(0, grouped0)
+        vote0 = votes(0, banks[0], q0, (0, 1))
+        q1 = quantize(1, grouped1)
+        vote1 = votes(1, banks[1], q1, (0, 1))
+        grouped2 = interleave(2, nc.vector.tensor_copy)
+        grouped3 = interleave(3, nc.vector.tensor_copy)
+        q2 = quantize(2, grouped2)
+        vote2 = votes(2, banks[2], q2, (0, 1))
+        q3 = quantize(3, grouped3)
+        vote3 = [votes(3, banks[3 + h], q3, (h,)) for h in range(2)]
 
-        codes2, scales2 = quantize_late(0)
-        for col in range(2):
-            for e in range(2):
-                turn(banks[0], col, pair_votes[0][e][:, col, :], e == 0, e == 1)
-        for h in range(2):
-            scores(banks[1 + h], codes2[:], scales2[:], h)
-        votes2 = [votes(banks[1 + h], 2, h) for h in range(2)]
-        for col in range(2):
-            for e in range(2):
-                turn(banks[0], 2 + col, pair_votes[1][e][:, col, :], e == 0, e == 1)
-
-        codes3, scales3 = quantize_late(1)
-        for h in range(2):
-            scores(banks[3 + h], codes3[:], scales3[:], h)
-        votes3 = [votes(banks[3 + h], 3, h) for h in range(2)]
-
+        for e, vote in enumerate((vote0, vote1)):
+            for col in range(4):
+                turn(banks[5], col, vote[:, col // 2, col % 2, :], e == 0 and col == 0, e == 1 and col == 3)
         nc.vector.tensor_reduce(
-            res[:].rearrange("p h e j -> p (h e) j")[:, :, 0:8],
-            banks[0][:].rearrange("p (b r u) -> p b r u", b=4, u=16),
+            res[:].rearrange("p h s j -> p (h s) j")[:, :, 0:8],
+            banks[5][:].rearrange("p (b r u) -> p b r u", b=4, u=16),
             AXIS_X,
             ADD,
         )
         for h in range(2):
-            for col in range(2):
-                turn(banks[5], 2 * h + col, votes2[h][:, col, :], True, True)
-        nc.vector.tensor_reduce(
-            res[:].rearrange("p h e j -> p (h e) j")[:, :, 8:12],
-            banks[5][:].rearrange("p (b r u) -> p b r u", b=4, u=SEG),
-            AXIS_X,
-            ADD,
-        )
+            for s in range(2):
+                turn(banks[6 + h], s, vote2[:, h, s, :], s == 0, False)
         for h in range(2):
-            bank = banks[6] if h == 0 else banks[1]
-            for col in range(2):
-                turn(bank, col, votes3[h][:, col, :], True, True)
+            for s in range(2):
+                turn(banks[6 + h], s, vote3[h][:, 0, s, :], False, s == 1)
             nc.vector.tensor_reduce(
-                res[:, h, :, 12:16],
-                bank[:, 0:HALF].rearrange("p (b r u) -> p b r u", b=2, u=SEG),
+                res[:, h, :, 8:16],
+                banks[6 + h][:, 0:HALF].rearrange("p (s r u) -> p s r u", s=2, u=16),
                 AXIS_X,
                 ADD,
             )
-            nc.sync.dma_start(out_rows[h], res[:, h].rearrange("p e j -> p (e j)"))
+            nc.sync.dma_start(out_rows[h], res[:, h].rearrange("p s j -> p (s j)"))

@@ -23,8 +23,7 @@ PACK = 4
 HALF = N // 2
 RUNS = NQ // SEG
 GAIN = 8.0
-WARM_EARLY = 20
-WARM_LATE = 6
+WARM = 18
 
 
 def tile_attend_tok_vote_topk_kernel(tc, qT, k_words, k_scales, th, offs, out):
@@ -34,10 +33,11 @@ def tile_attend_tok_vote_topk_kernel(tc, qT, k_words, k_scales, th, offs, out):
         ps = ctx.enter_context(tc.psum_pool(name="ps", bufs=1))
         banks = [ps.tile([P, 512], F32, name=f"bank{b}") for b in range(8)]
 
+        q_rows = qT[0].rearrange("(p j) q -> p j q", j=PACK)
+        raw = [sb.tile([P, PACK, 2 * P], F32, name=f"raw{c}") for c in range(2)]
+        nc.sync.dma_start(raw[0][:], q_rows[:, :, 0 : 2 * P])
         offsets = sb.tile([P, N // 16], U16, name="offsets")
         nc.sync.dma_start(offsets[:], offs)
-        pool_words = sb.tile([P, T], I32, name="pool_words")
-        nc.sync.dma_start(pool_words[:], k_words[0].rearrange("p t r -> p (t r)").bitcast(I32))
 
         pool_scales = sb.tile([P, T // 4], I32, name="pool_scales")
         nc.vector.memset(pool_scales[:], 0)
@@ -45,10 +45,9 @@ def tile_attend_tok_vote_topk_kernel(tc, qT, k_words, k_scales, th, offs, out):
         for r in range(4):
             nc.sync.dma_start(pool_scales[r:P:32, :], scale_rows[r:16:4, :])
 
-        q_rows = qT[0].rearrange("(p j) q -> p j q", j=PACK)
-        raw = [sb.tile([P, PACK, 2 * P], F32, name=f"raw{c}") for c in range(2)]
-        for c in range(2):
-            nc.sync.dma_start(raw[c][:], q_rows[:, :, 2 * P * c : 2 * P * (c + 1)])
+        pool_words = sb.tile([P, T], I32, name="pool_words")
+        nc.sync.dma_start(pool_words[:], k_words[0].rearrange("p t r -> p (t r)").bitcast(I32))
+        nc.sync.dma_start(raw[1][:], q_rows[:, :, 2 * P : 4 * P])
 
         th_raw = sb.tile([2, 2 * P], F32, name="th_raw")
         nc.scalar.dma_start(th_raw[:], th[0, 0].rearrange("(c q) -> c q", c=2))
@@ -56,6 +55,8 @@ def tile_attend_tok_vote_topk_kernel(tc, qT, k_words, k_scales, th, offs, out):
         nc.gpsimd.memset(th_rows[:], 0.0)
         ident = sb.tile([P, P], F32, name="ident")
         make_identity(nc, ident[:])
+        ident_bf = sb.tile([P, P], BF16, name="ident_bf")
+        make_identity(nc, ident_bf[:])
         warm = sb.tile([P, 1], F32, name="warm")
         nc.scalar.activation(warm[:], th_rows[:, 0:1], SIGMOID)
         nc.scalar.activation(
@@ -68,15 +69,9 @@ def tile_attend_tok_vote_topk_kernel(tc, qT, k_words, k_scales, th, offs, out):
             nc.tensor.transpose(banks[7][:, e * P : (e + 1) * P], th_rows[:, e * P : (e + 1) * P], ident[:])
         bias = sb.tile([P, 2, 2], F32, name="bias")
         nc.scalar.copy(bias[:], banks[7][:, 0 : 2 * P].rearrange("p (e c) -> p e c", e=2)[:, :, 0:2])
-        for w in range(WARM_EARLY):
-            nc.tensor.transpose(banks[6][:, (w % 4) * P : (w % 4 + 1) * P], th_rows[:, 0:P], ident[:])
-        for w in range(WARM_LATE):
-            nc.tensor.transpose(banks[6][:, (w % 4) * P : (w % 4 + 1) * P], raw[0][:, 0, 0:P], ident[:])
 
-        key_words = sb.tile([P, N], U32, name="key_words", align_bytes=64)
-        nc.vector.tensor_copy(key_words[:], pool_words[:].bitcast(U32).indirect(offsets[:]))
         key_scales = sb.tile([P, N], U8, name="key_scales", align_bytes=64)
-        nc.vector.tensor_copy(key_scales[:], pool_scales[:].bitcast(U8).indirect(offsets[:]))
+        key_words = [sb.tile([P, HALF], U32, name=f"key_words{h}", align_bytes=64) for h in range(2)]
 
         def interleave(t, copy):
             grouped = sb.tile([P, P, PACK], BF16, name=f"grouped{t}", align_bytes=64)
@@ -92,21 +87,23 @@ def tile_attend_tok_vote_topk_kernel(tc, qT, k_words, k_scales, th, offs, out):
             nc.vector.quantize_mx(out=codes[:].bitcast(FP8X4), scales=scales[:], in_=grouped[:].rearrange("p m j -> p (m j)"))
             return codes, scales
 
-        def votes(t, bank, quantized, halves):
-            cols = slice(halves[0] * HALF, (halves[-1] + 1) * HALF)
+        def scores(bank, quantized, h):
+            cols = slice(h * HALF, (h + 1) * HALF)
             nc.tensor.matmul_mx(
                 out=bank[:, cols],
                 lhsT=quantized[0][:].bitcast(FP8X4),
                 lhsT_scale=quantized[1][:],
-                rhs=key_words[:, cols].bitcast(FP8X4),
+                rhs=key_words[h][:].bitcast(FP8X4),
                 rhs_scale=key_scales[:, cols],
                 start=True,
                 stop=True,
             )
-            vote = sb.tile([P, len(halves), 2, P], F32, name=f"vote{t}_{halves[0]}")
+
+        def votes(t, bank, h, lanes):
+            vote = sb.tile([P, len(lanes), P], F32, name=f"vote{t}_{h}_{lanes[0]}")
             nc.scalar.activation(
                 vote[:],
-                bank[:, cols].rearrange("p (h k s) -> p h s k", h=len(halves), s=2),
+                bank[:, h * HALF : (h + 1) * HALF].rearrange("p (k s) -> p s k", s=2)[:, lanes[0] : lanes[-1] + 1],
                 SIGMOID,
                 bias=bias[:, t % 2, t // 2 : t // 2 + 1],
                 scale=GAIN,
@@ -119,38 +116,65 @@ def tile_attend_tok_vote_topk_kernel(tc, qT, k_words, k_scales, th, offs, out):
         res = sb.tile([P, 2, 2, RUNS], F32, name="res")
         out_rows = out[0].rearrange("(h p s) j -> h p (s j)", h=2, s=2)
 
-        grouped0 = interleave(0, nc.scalar.copy)
+        grouped0 = interleave(0, nc.vector.tensor_copy)
         grouped1 = interleave(1, nc.scalar.copy)
-        q0 = quantize(0, grouped0)
-        vote0 = votes(0, banks[0], q0, (0, 1))
-        q1 = quantize(1, grouped1)
-        vote1 = votes(1, banks[1], q1, (0, 1))
+        for w in range(WARM):
+            nc.tensor.transpose(
+                banks[6][:].bitcast(BF16)[:, (w % 4) * P : (w % 4 + 1) * P],
+                grouped0[:].rearrange("p m j -> p (m j)")[:, 0:P],
+                ident_bf[:],
+            )
+        early = [quantize(0, grouped0), quantize(1, grouped1)]
+        nc.vector.tensor_copy(key_scales[:], pool_scales[:].bitcast(U8).indirect(offsets[:]))
+        for h in range(2):
+            nc.vector.tensor_copy(key_words[h][:], pool_words[:].bitcast(U32).indirect(offsets[:, 16 * h : 16 * h + 16]))
+        for h in range(2):
+            for e in range(2):
+                scores(banks[2 * h + e], early[e], h)
+        early_votes = [[votes(e, banks[2 * h + e], h, (0, 1)) for e in range(2)] for h in range(2)]
+
         grouped2 = interleave(2, nc.vector.tensor_copy)
         grouped3 = interleave(3, nc.vector.tensor_copy)
         q2 = quantize(2, grouped2)
-        vote2 = votes(2, banks[2], q2, (0, 1))
         q3 = quantize(3, grouped3)
-        vote3 = [votes(3, banks[3 + h], q3, (h,)) for h in range(2)]
+        for h in range(2):
+            scores(banks[0], q2, h)
+        vote2 = [votes(2, banks[0], h, (0, 1)) for h in range(2)]
+        for h in range(2):
+            scores(banks[1 + h], q3, h)
+        vote3_low = votes(3, banks[1], 0, (0, 1))
+        vote3_high = [votes(3, banks[2], 1, (s,)) for s in range(2)]
 
-        for e, vote in enumerate((vote0, vote1)):
-            for col in range(4):
-                turn(banks[5], col, vote[:, col // 2, col % 2, :], e == 0 and col == 0, e == 1 and col == 3)
-        nc.vector.tensor_reduce(
-            res[:].rearrange("p h s j -> p (h s) j")[:, :, 0:8],
-            banks[5][:].rearrange("p (b r u) -> p b r u", b=4, u=16),
-            AXIS_X,
-            ADD,
-        )
         for h in range(2):
             for s in range(2):
-                turn(banks[6 + h], s, vote2[:, h, s, :], s == 0, False)
-        for h in range(2):
-            for s in range(2):
-                turn(banks[6 + h], s, vote3[h][:, 0, s, :], False, s == 1)
+                for e in range(2):
+                    turn(banks[4 + h], s, early_votes[h][e][:, s, :], e == 0, e == 1)
             nc.vector.tensor_reduce(
-                res[:, h, :, 8:16],
-                banks[6 + h][:, 0:HALF].rearrange("p (s r u) -> p s r u", s=2, u=16),
+                res[:, h, :, 0:8],
+                banks[4 + h][:, 0:HALF].rearrange("p (s r u) -> p s r u", s=2, u=16),
                 AXIS_X,
                 ADD,
             )
-            nc.sync.dma_start(out_rows[h], res[:, h].rearrange("p s j -> p (s j)"))
+        for s in range(2):
+            turn(banks[6], s, vote2[0][:, s, :], s == 0, False)
+        last_banks = (banks[7], banks[3])
+        for s in range(2):
+            turn(last_banks[s], 0, vote2[1][:, s, :], True, False)
+        for s in range(2):
+            turn(banks[6], s, vote3_low[:, s, :], False, s == 1)
+        nc.vector.tensor_reduce(
+            res[:, 0, :, 8:16],
+            banks[6][:, 0:HALF].rearrange("p (s r u) -> p s r u", s=2, u=16),
+            AXIS_X,
+            ADD,
+        )
+        nc.sync.dma_start(out_rows[0], res[:, 0].rearrange("p s j -> p (s j)"))
+        for s in range(2):
+            turn(last_banks[s], 0, vote3_high[s][:, 0, :], False, True)
+            nc.vector.tensor_reduce(
+                res[:, 1, s, 8:16],
+                last_banks[s][:, 0:P].rearrange("p (r u) -> p r u", u=16),
+                AXIS_X,
+                ADD,
+            )
+        nc.sync.dma_start(out_rows[1], res[:, 1].rearrange("p s j -> p (s j)"))

from contextlib import ExitStack

import concourse.mybir as mybir
from concourse.masks import make_identity

N, T, D, NQ, SEG = 512, 2048, 512, 512, 32
FLOPS = 2 * N * D * NQ

F32 = mybir.dt.float32
BF16 = mybir.dt.bfloat16
I32 = mybir.dt.int32
U32 = mybir.dt.uint32
U16 = mybir.dt.uint16
U8 = mybir.dt.uint8
FP8X4 = mybir.dt.float8_e4m3fn_x4
SIGMOID = mybir.ActivationFunctionType.Sigmoid
COPY = mybir.ActivationFunctionType.Copy
ADD = mybir.AluOpType.add
AXIS_X = mybir.AxisListType.X

P = 128
PACK = 4
HALF = N // 2
RUNS = NQ // SEG
GAIN = 8.0
WARM = 18


def tile_attend_tok_vote_topk_kernel(tc, qT, k_words, k_scales, th, offs, out):
    nc = tc.nc
    with ExitStack() as ctx:
        sb = ctx.enter_context(tc.tile_pool(name="sb", bufs=1))
        ps = ctx.enter_context(tc.psum_pool(name="ps", bufs=1))
        banks = [ps.tile([P, 512], F32, name=f"bank{b}") for b in range(8)]

        q_rows = qT[0].rearrange("(p j) q -> p j q", j=PACK)
        raw = [sb.tile([P, PACK, 2 * P], F32, name=f"raw{c}") for c in range(2)]
        nc.sync.dma_start(raw[0][:], q_rows[:, :, 0 : 2 * P])
        offsets = sb.tile([P, N // 16], U16, name="offsets")
        nc.sync.dma_start(offsets[:], offs)

        pool_scales = sb.tile([P, T // 4], I32, name="pool_scales")
        nc.vector.memset(pool_scales[:], 0)
        scale_rows = k_scales[0].bitcast(I32)
        for r in range(4):
            nc.sync.dma_start(pool_scales[r:P:32, :], scale_rows[r:16:4, :])

        pool_words = sb.tile([P, T], I32, name="pool_words")
        nc.sync.dma_start(pool_words[:], k_words[0].rearrange("p t r -> p (t r)").bitcast(I32))
        nc.sync.dma_start(raw[1][:], q_rows[:, :, 2 * P : 4 * P])

        th_raw = sb.tile([2, 2 * P], F32, name="th_raw")
        nc.scalar.dma_start(th_raw[:], th[0, 0].rearrange("(c q) -> c q", c=2))
        th_rows = sb.tile([P, 2 * P], F32, name="th_rows")
        nc.gpsimd.memset(th_rows[:], 0.0)
        ident = sb.tile([P, P], F32, name="ident")
        make_identity(nc, ident[:])
        ident_bf = sb.tile([P, P], BF16, name="ident_bf")
        make_identity(nc, ident_bf[:])
        warm = sb.tile([P, 1], F32, name="warm")
        nc.scalar.activation(warm[:], th_rows[:, 0:1], SIGMOID)
        nc.scalar.activation(
            th_rows[0:2, :].rearrange("c (e g i) -> c e g i", e=2, i=4),
            th_raw[:].rearrange("c (g e i) -> c e g i", e=2, i=4),
            COPY,
            scale=-GAIN,
        )
        for e in range(2):
            nc.tensor.transpose(banks[7][:, e * P : (e + 1) * P], th_rows[:, e * P : (e + 1) * P], ident[:])
        bias = sb.tile([P, 2, 2], F32, name="bias")
        nc.scalar.copy(bias[:], banks[7][:, 0 : 2 * P].rearrange("p (e c) -> p e c", e=2)[:, :, 0:2])

        key_scales = sb.tile([P, N], U8, name="key_scales", align_bytes=64)
        key_words = [sb.tile([P, HALF], U32, name=f"key_words{h}", align_bytes=64) for h in range(2)]

        def interleave(t, copy):
            grouped = sb.tile([P, P, PACK], BF16, name=f"grouped{t}", align_bytes=64)
            copy(
                grouped[:].rearrange("p (g i) j -> p g j i", i=4),
                raw[t // 2][:].rearrange("p j (g e i) -> p e g j i", e=2, i=4)[:, t % 2],
            )
            return grouped

        def quantize(t, grouped):
            codes = sb.tile([P, P], U32, name=f"codes{t}", align_bytes=64)
            scales = sb.tile([P, P], U8, name=f"scales{t}", align_bytes=64)
            nc.vector.quantize_mx(out=codes[:].bitcast(FP8X4), scales=scales[:], in_=grouped[:].rearrange("p m j -> p (m j)"))
            return codes, scales

        def scores(bank, quantized, h):
            cols = slice(h * HALF, (h + 1) * HALF)
            nc.tensor.matmul_mx(
                out=bank[:, cols],
                lhsT=quantized[0][:].bitcast(FP8X4),
                lhsT_scale=quantized[1][:],
                rhs=key_words[h][:].bitcast(FP8X4),
                rhs_scale=key_scales[:, cols],
                start=True,
                stop=True,
            )

        def votes(t, bank, h, lanes):
            vote = sb.tile([P, len(lanes), P], F32, name=f"vote{t}_{h}_{lanes[0]}")
            nc.scalar.activation(
                vote[:],
                bank[:, h * HALF : (h + 1) * HALF].rearrange("p (k s) -> p s k", s=2)[:, lanes[0] : lanes[-1] + 1],
                SIGMOID,
                bias=bias[:, t % 2, t // 2 : t // 2 + 1],
                scale=GAIN,
            )
            return vote

        def turn(bank, col, vote, start, stop):
            nc.tensor.matmul(bank[:, col * P : (col + 1) * P], lhsT=vote, rhs=ident[:], is_transpose=True, start=start, stop=stop)

        res = sb.tile([P, 2, 2, RUNS], F32, name="res")
        out_rows = out[0].rearrange("(h p s) j -> h p (s j)", h=2, s=2)

        grouped0 = interleave(0, nc.vector.tensor_copy)
        grouped1 = interleave(1, nc.scalar.copy)
        for w in range(WARM):
            nc.tensor.transpose(
                banks[6][:].bitcast(BF16)[:, (w % 4) * P : (w % 4 + 1) * P],
                grouped0[:].rearrange("p m j -> p (m j)")[:, 0:P],
                ident_bf[:],
            )
        early = [quantize(0, grouped0), quantize(1, grouped1)]
        nc.vector.tensor_copy(key_scales[:], pool_scales[:].bitcast(U8).indirect(offsets[:]))
        for h in range(2):
            nc.vector.tensor_copy(key_words[h][:], pool_words[:].bitcast(U32).indirect(offsets[:, 16 * h : 16 * h + 16]))
        for h in range(2):
            for e in range(2):
                scores(banks[2 * h + e], early[e], h)
        early_votes = [[votes(e, banks[2 * h + e], h, (0, 1)) for e in range(2)] for h in range(2)]

        grouped2 = interleave(2, nc.vector.tensor_copy)
        grouped3 = interleave(3, nc.vector.tensor_copy)
        q2 = quantize(2, grouped2)
        q3 = quantize(3, grouped3)
        for h in range(2):
            scores(banks[0], q2, h)
        vote2 = [votes(2, banks[0], h, (0, 1)) for h in range(2)]
        for h in range(2):
            scores(banks[1 + h], q3, h)
        vote3_low = votes(3, banks[1], 0, (0, 1))
        vote3_high = [votes(3, banks[2], 1, (s,)) for s in range(2)]

        for h in range(2):
            for s in range(2):
                for e in range(2):
                    turn(banks[4 + h], s, early_votes[h][e][:, s, :], e == 0, e == 1)
            nc.vector.tensor_reduce(
                res[:, h, :, 0:8],
                banks[4 + h][:, 0:HALF].rearrange("p (s r u) -> p s r u", s=2, u=16),
                AXIS_X,
                ADD,
            )
        for s in range(2):
            turn(banks[6], s, vote2[0][:, s, :], s == 0, False)
        last_banks = (banks[7], banks[3])
        for s in range(2):
            turn(last_banks[s], 0, vote2[1][:, s, :], True, False)
        for s in range(2):
            turn(banks[6], s, vote3_low[:, s, :], False, s == 1)
        nc.vector.tensor_reduce(
            res[:, 0, :, 8:16],
            banks[6][:, 0:HALF].rearrange("p (s r u) -> p s r u", s=2, u=16),
            AXIS_X,
            ADD,
        )
        nc.sync.dma_start(out_rows[0], res[:, 0].rearrange("p s j -> p (s j)"))
        for s in range(2):
            turn(last_banks[s], 0, vote3_high[s][:, 0, :], False, True)
            nc.vector.tensor_reduce(
                res[:, 1, s, 8:16],
                last_banks[s][:, 0:P].rearrange("p (r u) -> p r u", u=16),
                AXIS_X,
                ADD,
            )
        nc.sync.dma_start(out_rows[1], res[:, 1].rearrange("p s j -> p (s j)"))
